import numpy as np
import ml_dtypes


def mxq(x, axis, fmt="e4m3"):
    dtype, down = {"e4m3": (ml_dtypes.float8_e4m3fn, 7), "e5m2": (ml_dtypes.float8_e5m2, 14)}[fmt]
    v = np.moveaxis(np.asarray(x, np.float32).astype(ml_dtypes.bfloat16).astype(np.float64), axis, -1)
    blocks = v.reshape(v.shape[:-1] + (-1, 32))
    amax = np.abs(blocks).max(-1, keepdims=True)
    byte = np.maximum(np.where(amax > 0, np.frexp(amax)[1] - 1 + 127, 0) - down, 1)
    scale = np.exp2(byte - 127.0)
    codes = (blocks / scale).astype(np.float32).astype(dtype).astype(np.float64)
    return np.moveaxis((codes * scale).reshape(v.shape), -1, axis)


WIDE = False


def mx_kscale(k):
    if not WIDE:
        return np.ones(k)
    levels = np.array([10, -10, 5, -5, 0])
    if k % 512:
        return np.exp2(np.random.permutation(np.resize(levels, k // 32))).repeat(32)
    a = np.empty((k // 512, 16))
    for p in range(k // 512):
        a[p, :8] = np.random.permutation(np.resize(levels, 8))
        for g in range(8):
            far = levels[np.abs(levels - a[p, g]) >= 10]
            a[p, g + 8] = far[np.random.randint(len(far))]
    return np.exp2(a.ravel()).repeat(32)


def f64(x):
    return np.asarray(x).astype(np.float64)


def striped(idx):
    return np.tile(idx.reshape(-1, 16).T, (8, 1)).astype(np.uint16)


def unstriped(offs):
    return offs[:16].T.reshape(-1).astype(np.int64)


def pack_weight(w):
    k, n = w.shape
    w = f64(np.asarray(w, np.float32).astype(ml_dtypes.bfloat16)).reshape(k // 32, 32, n)
    amax = np.abs(w).max(1)
    byte = np.clip(np.where(amax > 0, np.frexp(amax)[1] - 1 + 127 - 7, 1), 1, 254)
    scaled = (w * np.exp2(127.0 - byte)[:, None, :]).reshape(k, n).astype(np.float32)
    words = np.ascontiguousarray(scaled.reshape(k // 512, 128, 4, n).transpose(0, 1, 3, 2)).astype(ml_dtypes.float8_e4m3fn).view(np.uint8)
    return words, np.ascontiguousarray(byte.astype(np.uint8).reshape(k // 512, 16, n))


def unpack_weight(words, scales):
    g, p, n, _ = words.shape
    vals = np.ascontiguousarray(words).view(ml_dtypes.float8_e4m3fn).astype(np.float64) * np.repeat(np.exp2(scales.astype(np.float64) - 127.0), 8, axis=1)[..., None]
    return vals.transpose(0, 1, 3, 2).reshape(g * 512, n)


K, T, S, N = 512, 2048, 1024, 128


def setup_inputs():
    n = np.random.standard_normal
    s = mx_kscale(K)[:, None]
    w1, w2 = n((2, K, N)) / np.sqrt(2 * K) / s[None]
    p1, p2 = pack_weight(w1), pack_weight(w2)
    return {
        "xT": (n((K, S)) * s).astype(np.float32),
        "sT": (n((K, T)) * s).astype(np.float32),
        "w1_words": p1[0],
        "w1_scales": p1[1],
        "w2_words": p2[0],
        "w2_scales": p2[1],
        "b": (0.3 * n((N, 1))).astype(np.float32),
        "offs": striped(np.random.permutation(T)[:S]),
    }


def reference(xT, sT, w1_words, w1_scales, w2_words, w2_scales, b, offs):
    y = unpack_weight(w1_words, w1_scales).T @ mxq(f64(xT), 0, "e4m3") + unpack_weight(w2_words, w2_scales).T @ mxq(f64(sT)[:, unstriped(offs)], 0, "e4m3")
    return y + f64(b)

@@ -1,0 +1,162 @@
+from contextlib import ExitStack
+
+import concourse.mybir as mybir
+
+K, T, S, N = 512, 2048, 1024, 128
+FLOPS = 2 * 2 * K * S * N
+
+F32 = mybir.dt.float32
+BF16 = mybir.dt.bfloat16
+I32 = mybir.dt.int32
+U32 = mybir.dt.uint32
+U16 = mybir.dt.uint16
+U8 = mybir.dt.uint8
+FP8X4 = mybir.dt.float8_e4m3fn_x4
+COPY = mybir.ActivationFunctionType.Copy
+IDENTITY = mybir.ActivationFunctionType.Identity
+
+P = 128
+SLICE = 256
+SLICES = S // SLICE
+
+
+def tile_picked_recall_bias_e_kernel(tc, xT, sT, w1_words, w1_scales, w2_words, w2_scales, b, offs, out):
+    nc = tc.nc
+    with ExitStack() as ctx:
+        keep = ctx.enter_context(tc.tile_pool(name="keep", bufs=1))
+        psum = ctx.enter_context(tc.psum_pool(name="psum", bufs=1))
+
+        offsets = keep.tile([P, S // 16], U16, name="offsets")
+        w1_codes = keep.tile([P, N], U32, name="w1_codes", align_bytes=64)
+        w2_codes = keep.tile([P, N], U32, name="w2_codes", align_bytes=64)
+        w_bytes = keep.tile([P, 2 * N], U8, name="w_bytes", align_bytes=64)
+        bias = keep.tile([P, 1], F32, name="bias")
+        warm = keep.tile([P, 1], F32, name="warm")
+
+        s_rows = sT.rearrange("(p t) w -> p t w", t=4)
+        x_rows = xT.rearrange("(p t) w -> p t w", t=4)
+        s_chunks = [(0, 0, 1024), (0, 1024, 2048), (1, 0, 1024), (1, 1024, 1536), (1, 1536, 2048)]
+        x_chunks = [(j * SLICE, (j + 1) * SLICE) for j in range(SLICES)]
+        s_raw = [keep.tile([P, 2, hi - lo], F32, name=f"s_raw{i}") for i, (u, lo, hi) in enumerate(s_chunks)]
+        x_raw = [keep.tile([P, 4, hi - lo], F32, name=f"x_raw{i}") for i, (lo, hi) in enumerate(x_chunks)]
+
+        def load_s(i):
+            u, lo, hi = s_chunks[i]
+            nc.sync.dma_start(s_raw[i][:], s_rows[:, 2 * u : 2 * u + 2, lo:hi])
+
+        def load_scales(side, quad):
+            scales = (w1_scales, w2_scales)[side]
+            nc.sync.dma_start(
+                w_bytes[32 * quad : 32 * quad + 4, side * N : (side + 1) * N].bitcast(I32),
+                scales[0, 4 * quad : 4 * quad + 4, :].bitcast(I32),
+            )
+
+        def load_codes(side):
+            codes, words = ((w1_codes, w1_words), (w2_codes, w2_words))[side]
+            nc.sync.dma_start(codes[:].bitcast(I32), words[0].rearrange("p n t -> p (n t)").bitcast(I32))
+
+        nc.gpsimd.memset(w_bytes[:], 0)
+        nc.gpsimd.memset(warm[:], 0.0)
+        nc.gpsimd.dma_start(bias[:], b)
+        nc.scalar.activation(warm[:], warm[:], IDENTITY)
+        load_s(0)
+        nc.sync.dma_start(offsets[:], offs)
+        for quad in range(4):
+            load_scales(1, quad)
+        load_s(1)
+        load_scales(0, 0)
+        load_s(2)
+        for quad in range(1, 4):
+            load_scales(0, quad)
+        load_s(3)
+        load_codes(1)
+        load_s(4)
+        load_codes(0)
+        for i, (lo, hi) in enumerate(x_chunks):
+            nc.sync.dma_start(x_raw[i][:], x_rows[:, :, lo:hi])
+
+        pairs = [keep.tile([P, 2 * T], BF16, name=f"pairs{u}", align_bytes=64) for u in range(2)]
+        picked = keep.tile([P, S, 4], BF16, name="picked", align_bytes=64)
+        x_grouped = keep.tile([P, S, 4], BF16, name="x_grouped", align_bytes=64)
+        s_codes = keep.tile([P, S], U32, name="s_codes", align_bytes=64)
+        s_bytes = keep.tile([P, S], U8, name="s_bytes", align_bytes=64)
+        x_codes = keep.tile([P, S], U32, name="x_codes", align_bytes=64)
+        x_bytes = keep.tile([P, S], U8, name="x_bytes", align_bytes=64)
+        result = keep.tile([P, S], F32, name="result", align_bytes=64)
+        banks = [psum.tile([P, SLICE], F32, name=f"bank{j}") for j in range(SLICES)]
+
+        def move(engine, dst, src):
+            if engine == "v":
+                nc.vector.tensor_copy(dst, src)
+            else:
+                nc.scalar.activation(dst, src, COPY)
+
+        def cast_s(engine, i, a, z):
+            u, lo, hi = s_chunks[i]
+            dst = pairs[u][:].rearrange("p (w e) -> p w e", e=2)[:, lo + a : lo + z, :]
+            move(engine, dst, s_raw[i][:, :, a:z].rearrange("p e w -> p w e"))
+
+        def cast_x(engine, i, a, z):
+            lo, hi = x_chunks[i]
+            move(engine, x_grouped[:, lo + a : lo + z, :], x_raw[i][:, :, a:z].rearrange("p t w -> p w t"))
+
+        def gather(u, a, z):
+            nc.vector.tensor_copy(
+                picked[:].bitcast(U32)[:, a:z, u],
+                pairs[u][:].bitcast(U32).indirect(offsets[:, a // 16 : z // 16]),
+            )
+
+        def quantize(grouped, codes, scale_bytes, lo, hi):
+            nc.vector.quantize_mx(
+                out=codes[:, lo:hi].bitcast(FP8X4),
+                scales=scale_bytes[:, lo:hi],
+                in_=grouped[:, lo:hi, :].rearrange("p w t -> p (w t)"),
+            )
+
+        def multiply(j, side, codes, scale_bytes, w_codes, start):
+            cols = slice(j * SLICE, (j + 1) * SLICE)
+            nc.tensor.matmul_mx(
+                out=banks[j][:],
+                lhsT=w_codes[:].bitcast(FP8X4),
+                lhsT_scale=w_bytes[:, side * N : (side + 1) * N],
+                rhs=codes[:, cols].bitcast(FP8X4),
+                rhs_scale=scale_bytes[:, cols],
+                start=start,
+                stop=not start,
+            )
+
+        def finish_s(lo, hi):
+            quantize(picked, s_codes, s_bytes, lo, hi)
+            for j in range(lo // SLICE, hi // SLICE):
+                multiply(j, 1, s_codes, s_bytes, w2_codes, True)
+
+        def finish_x(j):
+            cols = slice(j * SLICE, (j + 1) * SLICE)
+            quantize(x_grouped, x_codes, x_bytes, j * SLICE, (j + 1) * SLICE)
+            multiply(j, 0, x_codes, x_bytes, w1_codes, False)
+            nc.scalar.activation(result[:, cols], banks[j][:], IDENTITY, bias=bias[:])
+            nc.sync.dma_start(out[:, cols], result[:, cols])
+
+        cast_s("s", 0, 0, 512)
+        cast_s("v", 0, 512, 1024)
+        cast_s("s", 1, 0, 352)
+        cast_s("v", 1, 352, 1024)
+        gather(0, 0, S)
+        cast_s("s", 2, 0, 512)
+        cast_s("s", 2, 512, 1024)
+        cast_s("v", 3, 0, 512)
+        cast_s("s", 4, 0, 176)
+        cast_s("v", 4, 176, 512)
+        gather(1, 0, 512)
+        cast_x("s", 0, 0, 256)
+        gather(1, 512, 1024)
+        cast_x("s", 1, 0, 256)
+        finish_s(0, 512)
+        finish_x(0)
+        cast_x("s", 2, 0, 256)
+        finish_s(512, 1024)
+        finish_x(1)
+        cast_x("s", 3, 0, 96)
+        finish_x(2)
+        cast_x("v", 3, 96, 256)
+        finish_x(3)

@@ -18,6 +18,7 @@ IDENTITY = mybir.ActivationFunctionType.Identity
 P = 128
 SLICE = 256
 SLICES = S // SLICE
+HALF = S // 2
 
 
 def tile_picked_recall_bias_e_kernel(tc, xT, sT, w1_words, w1_scales, w2_words, w2_scales, b, offs, out):
@@ -36,7 +37,7 @@ def tile_picked_recall_bias_e_kernel(tc, xT, sT, w1_words, w1_scales, w2_words, 
         s_rows = sT.rearrange("(p t) w -> p t w", t=4)
         x_rows = xT.rearrange("(p t) w -> p t w", t=4)
         s_chunks = [(0, 0, 1024), (0, 1024, 2048), (1, 0, 1024), (1, 1024, 1536), (1, 1536, 2048)]
-        x_chunks = [(j * SLICE, (j + 1) * SLICE) for j in range(SLICES)]
+        x_chunks = [(lo, lo + SLICE) for lo in (0, 512, 256, 768)]
         s_raw = [keep.tile([P, 2, hi - lo], F32, name=f"s_raw{i}") for i, (u, lo, hi) in enumerate(s_chunks)]
         x_raw = [keep.tile([P, 4, hi - lo], F32, name=f"x_raw{i}") for i, (lo, hi) in enumerate(x_chunks)]
 
@@ -44,30 +45,29 @@ def tile_picked_recall_bias_e_kernel(tc, xT, sT, w1_words, w1_scales, w2_words, 
             u, lo, hi = s_chunks[i]
             nc.sync.dma_start(s_raw[i][:], s_rows[:, 2 * u : 2 * u + 2, lo:hi])
 
-        def load_scales(side, quad):
-            scales = (w1_scales, w2_scales)[side]
-            nc.sync.dma_start(
-                w_bytes[32 * quad : 32 * quad + 4, side * N : (side + 1) * N].bitcast(I32),
-                scales[0, 4 * quad : 4 * quad + 4, :].bitcast(I32),
-            )
-
         def load_codes(side):
             codes, words = ((w1_codes, w1_words), (w2_codes, w2_words))[side]
             nc.sync.dma_start(codes[:].bitcast(I32), words[0].rearrange("p n t -> p (n t)").bitcast(I32))
 
-        nc.gpsimd.memset(w_bytes[:], 0)
-        nc.gpsimd.memset(warm[:], 0.0)
-        nc.gpsimd.dma_start(bias[:], b)
+        nc.vector.memset(w_bytes[:].bitcast(I32), 0)
+        nc.vector.memset(warm[:], 0.0)
         nc.scalar.activation(warm[:], warm[:], IDENTITY)
+
+        def load_scales(side):
+            scales = (w1_scales, w2_scales)[side]
+            for quad in range(4):
+                nc.sync.dma_start(
+                    w_bytes[32 * quad : 32 * quad + 4, side * N : (side + 1) * N].bitcast(I32),
+                    scales[0, 4 * quad : 4 * quad + 4, :].bitcast(I32),
+                )
+
         load_s(0)
         nc.sync.dma_start(offsets[:], offs)
-        for quad in range(4):
-            load_scales(1, quad)
+        load_scales(1)
         load_s(1)
-        load_scales(0, 0)
+        nc.sync.dma_start(bias[:], b)
         load_s(2)
-        for quad in range(1, 4):
-            load_scales(0, quad)
+        load_scales(0)
         load_s(3)
         load_codes(1)
         load_s(4)
@@ -76,14 +76,14 @@ def tile_picked_recall_bias_e_kernel(tc, xT, sT, w1_words, w1_scales, w2_words, 
             nc.sync.dma_start(x_raw[i][:], x_rows[:, :, lo:hi])
 
         pairs = [keep.tile([P, 2 * T], BF16, name=f"pairs{u}", align_bytes=64) for u in range(2)]
-        picked = keep.tile([P, S, 4], BF16, name="picked", align_bytes=64)
-        x_grouped = keep.tile([P, S, 4], BF16, name="x_grouped", align_bytes=64)
-        s_codes = keep.tile([P, S], U32, name="s_codes", align_bytes=64)
-        s_bytes = keep.tile([P, S], U8, name="s_bytes", align_bytes=64)
-        x_codes = keep.tile([P, S], U32, name="x_codes", align_bytes=64)
-        x_bytes = keep.tile([P, S], U8, name="x_bytes", align_bytes=64)
-        result = keep.tile([P, S], F32, name="result", align_bytes=64)
-        banks = [psum.tile([P, SLICE], F32, name=f"bank{j}") for j in range(SLICES)]
+        picked = [keep.tile([P, HALF, 4], BF16, name=f"picked{h}", align_bytes=64) for h in range(2)]
+        s_codes = [keep.tile([P, HALF], U32, name=f"s_codes{h}", align_bytes=64) for h in range(2)]
+        s_bytes = [keep.tile([P, HALF], U8, name=f"s_bytes{h}", align_bytes=64) for h in range(2)]
+        x_grouped = [keep.tile([P, SLICE, 4], BF16, name=f"x_grouped{j}", align_bytes=64) for j in range(SLICES)]
+        x_codes = [keep.tile([P, SLICE], U32, name=f"x_codes{j}", align_bytes=64) for j in range(SLICES)]
+        x_bytes = [keep.tile([P, SLICE], U8, name=f"x_bytes{j}", align_bytes=64) for j in range(SLICES)]
+        result = [keep.tile([P, HALF], F32, name=f"result{h}", align_bytes=64) for h in range(2)]
+        banks = [psum.tile([P, HALF], F32, name=f"bank{h}") for h in range(2)]
 
         def move(engine, dst, src):
             if engine == "v":
@@ -96,67 +96,70 @@ def tile_picked_recall_bias_e_kernel(tc, xT, sT, w1_words, w1_scales, w2_words, 
             dst = pairs[u][:].rearrange("p (w e) -> p w e", e=2)[:, lo + a : lo + z, :]
             move(engine, dst, s_raw[i][:, :, a:z].rearrange("p e w -> p w e"))
 
-        def cast_x(engine, i, a, z):
-            lo, hi = x_chunks[i]
-            move(engine, x_grouped[:, lo + a : lo + z, :], x_raw[i][:, :, a:z].rearrange("p t w -> p w t"))
+        def cast_x(engine, j, a, z):
+            move(engine, x_grouped[j][:, a:z, :], x_raw[j][:, :, a:z].rearrange("p t w -> p w t"))
 
-        def gather(u, a, z):
+        def gather(u, h):
             nc.vector.tensor_copy(
-                picked[:].bitcast(U32)[:, a:z, u],
-                pairs[u][:].bitcast(U32).indirect(offsets[:, a // 16 : z // 16]),
+                picked[h][:].bitcast(U32)[:, :, u],
+                pairs[u][:].bitcast(U32).indirect(offsets[:, h * HALF // 16 : (h + 1) * HALF // 16]),
             )
 
-        def quantize(grouped, codes, scale_bytes, lo, hi):
+        def quantize(grouped, codes, scale_bytes):
             nc.vector.quantize_mx(
-                out=codes[:, lo:hi].bitcast(FP8X4),
-                scales=scale_bytes[:, lo:hi],
-                in_=grouped[:, lo:hi, :].rearrange("p w t -> p (w t)"),
+                out=codes[:].bitcast(FP8X4),
+                scales=scale_bytes[:],
+                in_=grouped[:].rearrange("p w t -> p (w t)"),
             )
-
-        def multiply(j, side, codes, scale_bytes, w_codes, start):
-            cols = slice(j * SLICE, (j + 1) * SLICE)
-            nc.tensor.matmul_mx(
-                out=banks[j][:],
-                lhsT=w_codes[:].bitcast(FP8X4),
-                lhsT_scale=w_bytes[:, side * N : (side + 1) * N],
-                rhs=codes[:, cols].bitcast(FP8X4),
-                rhs_scale=scale_bytes[:, cols],
-                start=start,
-                stop=not start,
-            )
-
-        def finish_s(lo, hi):
-            quantize(picked, s_codes, s_bytes, lo, hi)
-            for j in range(lo // SLICE, hi // SLICE):
-                multiply(j, 1, s_codes, s_bytes, w2_codes, True)
 
         def finish_x(j):
-            cols = slice(j * SLICE, (j + 1) * SLICE)
-            quantize(x_grouped, x_codes, x_bytes, j * SLICE, (j + 1) * SLICE)
-            multiply(j, 0, x_codes, x_bytes, w1_codes, False)
-            nc.scalar.activation(result[:, cols], banks[j][:], IDENTITY, bias=bias[:])
-            nc.sync.dma_start(out[:, cols], result[:, cols])
+            h, i = j % 2, j // 2
+            cols = slice(i * SLICE, (i + 1) * SLICE)
+            quantize(x_grouped[j], x_codes[j], x_bytes[j])
+            nc.tensor.matmul_mx(
+                out=banks[h][:, cols],
+                lhsT=w2_codes[:].bitcast(FP8X4),
+                lhsT_scale=w_bytes[:, N : 2 * N],
+                rhs=s_codes[h][:, cols].bitcast(FP8X4),
+                rhs_scale=s_bytes[h][:, cols],
+                start=True,
+                stop=False,
+            )
+            nc.tensor.matmul_mx(
+                out=banks[h][:, cols],
+                lhsT=w1_codes[:].bitcast(FP8X4),
+                lhsT_scale=w_bytes[:, 0:N],
+                rhs=x_codes[j][:].bitcast(FP8X4),
+                rhs_scale=x_bytes[j][:],
+                start=False,
+                stop=True,
+            )
+
+        def store(h):
+            nc.scalar.activation(result[h][:], banks[h][:], IDENTITY, bias=bias[:])
+            nc.sync.dma_start(out[:, h * HALF : (h + 1) * HALF], result[h][:])
 
         cast_s("s", 0, 0, 512)
         cast_s("v", 0, 512, 1024)
         cast_s("s", 1, 0, 352)
         cast_s("v", 1, 352, 1024)
-        gather(0, 0, S)
+        gather(0, 0)
+        gather(0, 1)
         cast_s("s", 2, 0, 512)
         cast_s("s", 2, 512, 1024)
         cast_s("v", 3, 0, 512)
         cast_s("s", 4, 0, 176)
         cast_s("v", 4, 176, 512)
-        gather(1, 0, 512)
-        cast_x("s", 0, 0, 256)
-        gather(1, 512, 1024)
-        cast_x("s", 1, 0, 256)
-        finish_s(0, 512)
+        gather(1, 0)
+        gather(1, 1)
+        for j in range(3):
+            cast_x("s", j, 0, 256)
+        quantize(picked[0], s_codes[0], s_bytes[0])
         finish_x(0)
-        cast_x("s", 2, 0, 256)
-        finish_s(512, 1024)
+        quantize(picked[1], s_codes[1], s_bytes[1])
         finish_x(1)
-        cast_x("s", 3, 0, 96)
         finish_x(2)
-        cast_x("v", 3, 96, 256)
+        store(0)
+        cast_x("v", 3, 0, 256)
         finish_x(3)
+        store(1)

from contextlib import ExitStack

import concourse.mybir as mybir

K, T, S, N = 512, 2048, 1024, 128
FLOPS = 2 * 2 * K * S * N

F32 = mybir.dt.float32
BF16 = mybir.dt.bfloat16
I32 = mybir.dt.int32
U32 = mybir.dt.uint32
U16 = mybir.dt.uint16
U8 = mybir.dt.uint8
FP8X4 = mybir.dt.float8_e4m3fn_x4
COPY = mybir.ActivationFunctionType.Copy
IDENTITY = mybir.ActivationFunctionType.Identity

P = 128
SLICE = 256
SLICES = S // SLICE
HALF = S // 2


def tile_picked_recall_bias_e_kernel(tc, xT, sT, w1_words, w1_scales, w2_words, w2_scales, b, offs, out):
    nc = tc.nc
    with ExitStack() as ctx:
        keep = ctx.enter_context(tc.tile_pool(name="keep", bufs=1))
        psum = ctx.enter_context(tc.psum_pool(name="psum", bufs=1))

        offsets = keep.tile([P, S // 16], U16, name="offsets")
        w1_codes = keep.tile([P, N], U32, name="w1_codes", align_bytes=64)
        w2_codes = keep.tile([P, N], U32, name="w2_codes", align_bytes=64)
        w_bytes = keep.tile([P, 2 * N], U8, name="w_bytes", align_bytes=64)
        bias = keep.tile([P, 1], F32, name="bias")
        warm = keep.tile([P, 1], F32, name="warm")

        s_rows = sT.rearrange("(p t) w -> p t w", t=4)
        x_rows = xT.rearrange("(p t) w -> p t w", t=4)
        s_chunks = [(0, 0, 1024), (0, 1024, 2048), (1, 0, 1024), (1, 1024, 1536), (1, 1536, 2048)]
        x_chunks = [(lo, lo + SLICE) for lo in (0, 512, 256, 768)]
        s_raw = [keep.tile([P, 2, hi - lo], F32, name=f"s_raw{i}") for i, (u, lo, hi) in enumerate(s_chunks)]
        x_raw = [keep.tile([P, 4, hi - lo], F32, name=f"x_raw{i}") for i, (lo, hi) in enumerate(x_chunks)]

        def load_s(i):
            u, lo, hi = s_chunks[i]
            nc.sync.dma_start(s_raw[i][:], s_rows[:, 2 * u : 2 * u + 2, lo:hi])

        def load_codes(side):
            codes, words = ((w1_codes, w1_words), (w2_codes, w2_words))[side]
            nc.sync.dma_start(codes[:].bitcast(I32), words[0].rearrange("p n t -> p (n t)").bitcast(I32))

        nc.vector.memset(w_bytes[:].bitcast(I32), 0)
        nc.vector.memset(warm[:], 0.0)
        nc.scalar.activation(warm[:], warm[:], IDENTITY)

        def load_scales(side):
            scales = (w1_scales, w2_scales)[side]
            for quad in range(4):
                nc.sync.dma_start(
                    w_bytes[32 * quad : 32 * quad + 4, side * N : (side + 1) * N].bitcast(I32),
                    scales[0, 4 * quad : 4 * quad + 4, :].bitcast(I32),
                )

        load_s(0)
        nc.sync.dma_start(offsets[:], offs)
        load_scales(1)
        load_s(1)
        nc.sync.dma_start(bias[:], b)
        load_s(2)
        load_scales(0)
        load_s(3)
        load_codes(1)
        load_s(4)
        load_codes(0)
        for i, (lo, hi) in enumerate(x_chunks):
            nc.sync.dma_start(x_raw[i][:], x_rows[:, :, lo:hi])

        pairs = [keep.tile([P, 2 * T], BF16, name=f"pairs{u}", align_bytes=64) for u in range(2)]
        picked = [keep.tile([P, HALF, 4], BF16, name=f"picked{h}", align_bytes=64) for h in range(2)]
        s_codes = [keep.tile([P, HALF], U32, name=f"s_codes{h}", align_bytes=64) for h in range(2)]
        s_bytes = [keep.tile([P, HALF], U8, name=f"s_bytes{h}", align_bytes=64) for h in range(2)]
        x_grouped = [keep.tile([P, SLICE, 4], BF16, name=f"x_grouped{j}", align_bytes=64) for j in range(SLICES)]
        x_codes = [keep.tile([P, SLICE], U32, name=f"x_codes{j}", align_bytes=64) for j in range(SLICES)]
        x_bytes = [keep.tile([P, SLICE], U8, name=f"x_bytes{j}", align_bytes=64) for j in range(SLICES)]
        result = [keep.tile([P, HALF], F32, name=f"result{h}", align_bytes=64) for h in range(2)]
        banks = [psum.tile([P, HALF], F32, name=f"bank{h}") for h in range(2)]

        def move(engine, dst, src):
            if engine == "v":
                nc.vector.tensor_copy(dst, src)
            else:
                nc.scalar.activation(dst, src, COPY)

        def cast_s(engine, i, a, z):
            u, lo, hi = s_chunks[i]
            dst = pairs[u][:].rearrange("p (w e) -> p w e", e=2)[:, lo + a : lo + z, :]
            move(engine, dst, s_raw[i][:, :, a:z].rearrange("p e w -> p w e"))

        def cast_x(engine, j, a, z):
            move(engine, x_grouped[j][:, a:z, :], x_raw[j][:, :, a:z].rearrange("p t w -> p w t"))

        def gather(u, h):
            nc.vector.tensor_copy(
                picked[h][:].bitcast(U32)[:, :, u],
                pairs[u][:].bitcast(U32).indirect(offsets[:, h * HALF // 16 : (h + 1) * HALF // 16]),
            )

        def quantize(grouped, codes, scale_bytes):
            nc.vector.quantize_mx(
                out=codes[:].bitcast(FP8X4),
                scales=scale_bytes[:],
                in_=grouped[:].rearrange("p w t -> p (w t)"),
            )

        def finish_x(j):
            h, i = j % 2, j // 2
            cols = slice(i * SLICE, (i + 1) * SLICE)
            quantize(x_grouped[j], x_codes[j], x_bytes[j])
            nc.tensor.matmul_mx(
                out=banks[h][:, cols],
                lhsT=w2_codes[:].bitcast(FP8X4),
                lhsT_scale=w_bytes[:, N : 2 * N],
                rhs=s_codes[h][:, cols].bitcast(FP8X4),
                rhs_scale=s_bytes[h][:, cols],
                start=True,
                stop=False,
            )
            nc.tensor.matmul_mx(
                out=banks[h][:, cols],
                lhsT=w1_codes[:].bitcast(FP8X4),
                lhsT_scale=w_bytes[:, 0:N],
                rhs=x_codes[j][:].bitcast(FP8X4),
                rhs_scale=x_bytes[j][:],
                start=False,
                stop=True,
            )

        def store(h):
            nc.scalar.activation(result[h][:], banks[h][:], IDENTITY, bias=bias[:])
            nc.sync.dma_start(out[:, h * HALF : (h + 1) * HALF], result[h][:])

        cast_s("s", 0, 0, 512)
        cast_s("v", 0, 512, 1024)
        cast_s("s", 1, 0, 352)
        cast_s("v", 1, 352, 1024)
        gather(0, 0)
        gather(0, 1)
        cast_s("s", 2, 0, 512)
        cast_s("s", 2, 512, 1024)
        cast_s("v", 3, 0, 512)
        cast_s("s", 4, 0, 176)
        cast_s("v", 4, 176, 512)
        gather(1, 0)
        gather(1, 1)
        for j in range(3):
            cast_x("s", j, 0, 256)
        quantize(picked[0], s_codes[0], s_bytes[0])
        finish_x(0)
        quantize(picked[1], s_codes[1], s_bytes[1])
        finish_x(1)
        finish_x(2)
        store(0)
        cast_x("v", 3, 0, 256)
        finish_x(3)
        store(1)
